import numpy as np, ml_dtypes
CORES = [66,74,82,90,194,202,210,218]
N = 8
F = 32
B1, B2, LR, EPS = 0.75, 0.875, 2.0, 0.001
def setup_inputs(rng):
    idle = rng.random((128, N * F)) < 0.125; ib = np.stack([idle[:, F * r:F * r + F] for r in range(N)])
    return {"gr": (rng.standard_normal((N, 128, N * F), dtype=np.float32) * ~idle).astype(ml_dtypes.bfloat16), "m": (rng.standard_normal((N, 128, F), dtype=np.float32) * np.where(ib, 0.004, 1.0)).astype(ml_dtypes.bfloat16), "v": np.where(ib, 2e-6 * 50 ** rng.random((N, 128, F)), (0.5 + rng.standard_normal((N, 128, F), dtype=np.float32) ** 2) * N).astype(ml_dtypes.bfloat16), "w": rng.standard_normal((N, 128, F), dtype=np.float32).astype(ml_dtypes.bfloat16)}
def setup_inputs_big(rng):
    d = setup_inputs(rng)
    for k in ("gr", "m", "v", "w"): d[k] = (d[k].astype(np.float32) * 1024.0).astype(d[k].dtype)
    return d
def setup_inputs_small(rng):
    d = setup_inputs(rng)
    for k in ("gr", "m", "v", "w"): d[k] = (d[k].astype(np.float32) * (1 / 1024.0)).astype(d[k].dtype)
    return d
def setup_inputs_apart(rng):
    d = setup_inputs(rng)
    f = (10.0 ** rng.permutation(np.linspace(-1.5, 1.5, N))).astype(np.float32).reshape(N, 1, 1)
    for k in ("gr", "m", "v", "w"): d[k] = (d[k].astype(np.float32) * f).astype(d[k].dtype)
    return d
def reference(gr, m, v, w):
    GR, M, V, W = gr.astype(np.float64), m.astype(np.float64), v.astype(np.float64), w.astype(np.float64)
    s = GR.sum(axis=0)
    sb = np.stack([s[:, F * r:F * r + F] for r in range(N)])
    m2 = B1 * M + (1 - B1) * sb
    v2 = B2 * V + (1 - B2) * sb ** 2
    w2 = W - LR * m2 / (np.sqrt(v2) + EPS)
    return {"y": np.broadcast_to(np.concatenate(list(w2), axis=1).astype(ml_dtypes.bfloat16), (N, 128, N * F)), "mo": m2.astype(ml_dtypes.bfloat16), "vo": v2.astype(ml_dtypes.bfloat16)}

import math
from concourse.bass import DstId, RemoteDMATransfer
from concourse.mybir import AluOpType, ActivationFunctionType

N, F, P = 8, 32, 128
B1, B2, EPS = 0.75, 0.875, 0.001
TINY = 1e-12

_F32 = ["a", "ra", "ea", "m75", "pm", "v875", "t", "mm", "u", "h", "d", "rc", "z", "sq"]
SCRATCH = {
    "grs": ("sbuf", [P, N * F], "bfloat16"),
    "land": ("sbuf", [P, N * F], "bfloat16"),
    "yb": ("sbuf", [P, N * F], "bfloat16"),
    "vs": ("sbuf", [P, F], "bfloat16"),
    "ms": ("sbuf", [P, F], "bfloat16"),
    "ws": ("sbuf", [P, F], "bfloat16"),
    "mob": ("sbuf", [P, F], "bfloat16"),
    "vob": ("sbuf", [P, F], "bfloat16"),
    "idn": ("sbuf", [P, P], "bfloat16"),
    "q": ("psum", [P, F], "float32"),
}
for _n in _F32:
    SCRATCH[_n] = ("sbuf", [P, F], "float32")

SEMAPHORES = (["ld_g", "ld_v", "ld_m", "ld_w", "fill_ok", "id_ok", "q_ok", "ag", "lsem", "st_y", "st_mv",
               "mo_ok", "vo_ok", "w_ok"]
              + ["rs%d" % j for j in range(N)] + ["%s_ok" % n for n in _F32])


def _bits(mask):
    return [1 << b for b in range(mask.bit_length()) if (mask >> b) & 1]


def rank_program(g, core, T, topo):
    r = T.rank_of(core)
    if r is None:
        return
    S = T.sem
    cores = list(T.cores)
    V, A, PE, SY = g.vector, g.scalar, g.tensor, g.sync
    mult, add, sub = AluOpType.mult, AluOpType.add, AluOpType.subtract
    Sqrt, Square = ActivationFunctionType.Sqrt, ActivationFunctionType.Square

    def blk(t, j):
        return t[:, j * F:(j + 1) * F]

    def links(a, b):
        return 1 if (topo.mates(a, b) or topo.same_plane(a, b)) else 2

    def dst_id(j):
        rid, pid = topo.addr(cores[j], core)
        return DstId(rid=rid, pnc=pid)

    others = [j for j in range(N) if j != r]
    far_first = sorted(others, key=lambda j: -links(core, cores[j]))
    near_first = sorted(others, key=lambda j: links(cores[j], core))

    SY.dma_start(T.grs[:], T.gr[:]).then_inc(S.ld_g, 16)
    SY.dma_start(T.vs[:], T.v[:]).then_inc(S.ld_v, 16)
    SY.dma_start(T.ms[:], T.m[:]).then_inc(S.ld_m, 16)
    SY.dma_start(T.ws[:], T.w[:]).then_inc(S.ld_w, 16)

    rs, used = [], 0
    for j in far_first:
        eng = [b for b in _bits(topo.mask(core, cores[j])) if not (b & used)][0]
        used |= eng
        rs.append(RemoteDMATransfer(dst_ids=[dst_id(j)], dma_engine_mask=eng, remote_sem=S["rs%d" % r],
                                    src=blk(T.grs, j), dst=blk(T.land, r)))
    common = topo.mask(core, cores[others[0]])
    for j in others:
        common &= topo.mask(core, cores[j])
    cb = _bits(common)
    k = 1
    while k * 2 <= len(cb) and P % (k * 2) == 0:
        k *= 2
    ag_mask = sum(cb[:k])
    ag = RemoteDMATransfer(dst_ids=[dst_id(j) for j in far_first], dma_engine_mask=ag_mask, remote_sem=S.ag,
                           srcs=[blk(T.yb, r)], dsts=[blk(T.yb, r) for _ in far_first])
    left = len(rs) + k

    g.wait_ge(S.ld_g, 16)
    g.remote_dma_fused(rs, local_sem=S.lsem)
    g.wait_ge(S.fill_ok, 1)
    g.affine_select(T.idn[:], T.idn[:], [[-1, P]], AluOpType.is_equal, 0.0, 0, 1).then_inc(S.id_ok, 1)
    g.wait_ge(S.w_ok, 1)
    g.remote_dma_fused([ag], local_sem=S.lsem)
    g.wait_ge(S.lsem, left)

    PE.wait_ge(S.id_ok, 1)
    PE.wait_ge(S.ld_g, 16)
    PE.matmul(T.q[:], T.idn[:], blk(T.grs, r), True, False)
    for j in near_first[:-1]:
        PE.wait_ge(S["rs%d" % j], 1)
        PE.matmul(T.q[:], T.idn[:], blk(T.land, j), False, False)
    PE.wait_ge(S["rs%d" % near_first[-1]], 1)
    PE.matmul(T.q[:], T.idn[:], blk(T.land, near_first[-1]), False, True).then_inc(S.q_ok, 1)

    V.memset(T.idn[:], 0.25).then_inc(S.fill_ok, 1)
    V.wait_ge(S.ld_m, 16)
    V.tensor_scalar(T.m75[:], T.ms[:], B1, None, mult).then_inc(S.m75_ok, 1)
    V.wait_ge(S.ld_v, 16)
    V.tensor_scalar(T.v875[:], T.vs[:], B2, None, mult).then_inc(S.v875_ok, 1)
    V.wait_ge(S.a_ok, 1)
    V.reciprocal(T.ra[:], T.a[:]).then_inc(S.ra_ok, 1)
    V.wait_ge(S.ra_ok, 1)
    V.tensor_scalar(T.ea[:], T.ra[:], 0.5 * EPS, None, mult).then_inc(S.ea_ok, 1)
    V.wait_ge(S.m75_ok, 1)
    V.tensor_tensor(T.pm[:], T.m75[:], T.ra[:], mult).then_inc(S.pm_ok, 1)
    V.wait_ge(S.ea_ok, 1)
    V.wait_ge(S.pm_ok, 1)
    V.wait_ge(S.v875_ok, 1)
    V.wait_ge(S.ld_w, 16)
    V.wait_ge(S.q_ok, 1)
    V.tensor_tensor(T.t[:], T.q[:], T.ra[:], mult).then_inc(S.t_ok, 1)
    V.wait_ge(S.t_ok, 1)
    V.tensor_tensor(T.mm[:], T.t[:], T.pm[:], add).then_inc(S.mm_ok, 1)
    V.tensor_tensor(T.mob[:], T.q[:], T.m75[:], add).then_inc(S.mo_ok, 1)
    V.wait_ge(S.h_ok, 1)
    V.tensor_tensor(T.d[:], T.h[:], T.ea[:], add).then_inc(S.d_ok, 1)
    V.wait_ge(S.d_ok, 1)
    V.reciprocal(T.rc[:], T.d[:]).then_inc(S.rc_ok, 1)
    V.wait_ge(S.rc_ok, 1)
    V.wait_ge(S.mm_ok, 1)
    V.tensor_tensor(T.z[:], T.rc[:], T.mm[:], mult).then_inc(S.z_ok, 1)
    V.wait_ge(S.z_ok, 1)
    V.tensor_tensor(blk(T.yb, r), T.ws[:], T.z[:], sub).then_inc(S.w_ok, 1)
    V.wait_ge(S.sq_ok, 1)
    V.tensor_tensor(T.vob[:], T.sq[:], T.v875[:], add).then_inc(S.vo_ok, 1)

    A.wait_ge(S.ld_v, 16)
    A.activation(T.a[:], T.vs[:], Sqrt, bias=TINY, scale=B2).then_inc(S.a_ok, 1)
    A.wait_ge(S.t_ok, 1)
    A.activation(T.u[:], T.t[:], Square, scale=math.sqrt(0.5)).then_inc(S.u_ok, 1)
    A.wait_ge(S.u_ok, 1)
    A.activation(T.h[:], T.u[:], Sqrt, bias=0.25).then_inc(S.h_ok, 1)
    A.wait_ge(S.mo_ok, 1)
    A.activation(T.sq[:], T.q[:], Square, scale=math.sqrt(2.0)).then_inc(S.sq_ok, 1)
    A.wait_ge(S.lsem, left)
    A.dma_start(T.mo[:], T.mob[:]).then_inc(S.st_mv, 16)
    A.wait_ge(S.vo_ok, 1)
    A.dma_start(T.vo[:], T.vob[:]).then_inc(S.st_mv, 16)
    A.wait_ge(S.st_mv, 32)

    SY.wait_ge(S.w_ok, 1)
    SY.wait_ge(S.ag, k * len(others))
    SY.dma_start(T.y[:], T.yb[:]).then_inc(S.st_y, 16)
    SY.wait_ge(S.st_y, 16)
